import numpy as np
CORES = [26,90,154,218,282,346,410,474]
N = 8
ROOT = 6
def setup_inputs(rng):
    return {"x": rng.standard_normal((N, 128, 256), dtype=np.float32)}
def reference(x):
    y = np.full(x.shape, np.nan, x.dtype)
    y[ROOT] = x.max(axis=0)
    return {"y": y}

from concourse.bass import DstId, RemoteDMATransfer

PIECES = 4
ROWS, COLS = 128, 256
SLOT = [ROWS, COLS // PIECES]
CABLE = PIECES
MAX = 2

SCRATCH = {
    "xs": ("dram", [PIECES] + SLOT, "float32"),
    "land": ("dram", [PIECES + 1] + SLOT, "float32"),
}
SEMAPHORES = ["loaded", "sent", "arrived", "stored"]


def plan(T, topo):
    cores = list(T.cores)
    root = cores[T.root]
    helper = root ^ 1
    near = [c for c in cores if topo.rack(topo.host(c)) == topo.rack(topo.host(root))]
    far = [c for c in cores if c not in near]
    near_own = []
    for c in far:
        across = (3 - topo.host(c)) * 128 + c % 128
        near_own.append(helper if across == root else across)
    return root, far, near, list(far), near_own


def engines(mask):
    return bin(mask).count("1")


def rank_program(g, core, T, topo):
    root, far, near, far_own, near_own = plan(T, topo)
    if core in far:
        group, owners = far, far_own
    elif core in near or core in near_own:
        group, owners = near, near_own
    else:
        return
    sem = T.sem
    sent = 0

    def mask_to(dst):
        return topo.mask(core, dst)

    def fold(dst, out_ap, srcs):
        rid, pid = topo.addr(dst, core)
        g.remote_dma_fused(
            [RemoteDMATransfer(dst_ids=[DstId(rid=rid, pnc=pid)], dma_engine_mask=mask_to(dst), remote_sem=sem.arrived,
                               srcs=srcs, dsts=[out_ap], alu_op=MAX)],
            local_sem=sem.sent)
        return engines(mask_to(dst))

    if core in group:
        me = group.index(core)
        g.sync.dma_start(T.xs[:], T.x[:]).then_inc(sem.loaded, 16)
        g.wait_ge(sem.loaded, 16)
        for k in range(1, PIECES + 1):
            q = (me + k) % PIECES
            dst = owners[q]
            if dst == core:
                continue
            rid, pid = topo.addr(dst, core)
            g.remote_dma(T.land[me], T.xs[q], remote_sem=sem.arrived, local_sem=sem.sent, pid=pid, routing_id=rid,
                         dma_engine_mask=mask_to(dst))
            sent += engines(mask_to(dst))

    if core in owners:
        q = owners.index(core)
        srcs, due = [], 0
        for i, c in enumerate(group):
            if c == core:
                srcs.append(T.xs[q])
            else:
                srcs.append(T.land[i])
                due += engines(topo.mask(c, core))
        if owners is near_own:
            srcs.append(T.land[CABLE])
            due += engines(topo.mask(far_own[q], core))
            dst, out_ap = root, T.land[q]
        else:
            dst, out_ap = near_own[q], T.land[CABLE]
        g.wait_ge(sem.arrived, due)
        sent += fold(dst, out_ap, srcs)

    if core == root:
        due = sum(engines(topo.mask(c, root)) for c in near_own)
        g.sync.wait_ge(sem.arrived, due)
        g.sync.dma_start(T.y[:], T.land[0:PIECES]).then_inc(sem.stored, 16)
        g.sync.wait_ge(sem.stored, 16)

    g.wait_ge(sem.sent, sent)
